import numpy as np
import ml_dtypes


def mxq(x, axis, fmt="e4m3"):
    dtype, down = {"e4m3": (ml_dtypes.float8_e4m3fn, 7), "e5m2": (ml_dtypes.float8_e5m2, 14)}[fmt]
    v = np.moveaxis(np.asarray(x, np.float32).astype(ml_dtypes.bfloat16).astype(np.float64), axis, -1)
    blocks = v.reshape(v.shape[:-1] + (-1, 32))
    amax = np.abs(blocks).max(-1, keepdims=True)
    byte = np.maximum(np.where(amax > 0, np.frexp(amax)[1] - 1 + 127, 0) - down, 1)
    scale = np.exp2(byte - 127.0)
    codes = (blocks / scale).astype(np.float32).astype(dtype).astype(np.float64)
    return np.moveaxis((codes * scale).reshape(v.shape), -1, axis)


WIDE = False


def mx_kscale(k):
    if not WIDE:
        return np.ones(k)
    levels = np.array([10, -10, 5, -5, 0])
    if k % 512:
        return np.exp2(np.random.permutation(np.resize(levels, k // 32))).repeat(32)
    a = np.empty((k // 512, 16))
    for p in range(k // 512):
        a[p, :8] = np.random.permutation(np.resize(levels, 8))
        for g in range(8):
            far = levels[np.abs(levels - a[p, g]) >= 10]
            a[p, g + 8] = far[np.random.randint(len(far))]
    return np.exp2(a.ravel()).repeat(32)


def f64(x):
    return np.asarray(x).astype(np.float64)


def striped8(idx):
    return np.concatenate([x.reshape(-1, 16).T for x in idx]).astype(np.uint16)


def runs(offs, k):
    lists = np.stack([offs[16 * r : 16 * r + 16].T.reshape(-1) for r in range(8)]).astype(np.int64)
    return lists[np.arange(k) % 512 // 64]


def pack_weight(w):
    k, n = w.shape
    w = f64(np.asarray(w, np.float32).astype(ml_dtypes.bfloat16)).reshape(k // 32, 32, n)
    amax = np.abs(w).max(1)
    byte = np.clip(np.where(amax > 0, np.frexp(amax)[1] - 1 + 127 - 7, 1), 1, 254)
    scaled = (w * np.exp2(127.0 - byte)[:, None, :]).reshape(k, n).astype(np.float32)
    words = np.ascontiguousarray(scaled.reshape(k // 512, 128, 4, n).transpose(0, 1, 3, 2)).astype(ml_dtypes.float8_e4m3fn).view(np.uint8)
    return words, np.ascontiguousarray(byte.astype(np.uint8).reshape(k // 512, 16, n))


def unpack_weight(words, scales):
    g, p, n, _ = words.shape
    vals = np.ascontiguousarray(words).view(ml_dtypes.float8_e4m3fn).astype(np.float64) * np.repeat(np.exp2(scales.astype(np.float64) - 127.0), 8, axis=1)[..., None]
    return vals.transpose(0, 1, 3, 2).reshape(g * 512, n)

def planes(y):
    n, m = y.shape
    v = y.astype(np.float32).astype(ml_dtypes.bfloat16).astype(np.float64).reshape(n // 32, 32, m)
    top = np.abs(v).max(1)
    byte = np.clip(np.where(top > 0, np.frexp(top)[1] - 1 + 127 - 7, 1), 1, 254)
    codes = (v * np.exp2(127.0 - byte)[:, None, :]).reshape(n, m).astype(np.float32).astype(ml_dtypes.float8_e4m3fn).view(np.uint8)
    words = codes.reshape(n // 512, 128, 4, m).transpose(0, 1, 3, 2)
    return np.ascontiguousarray(words), np.ascontiguousarray(byte.astype(np.uint8).reshape(n // 512, 16, m))


K, T, S, H, W, C, J = 512, 2048, 512, 512, 256, 512, 512


def setup_inputs():
    n = np.random.standard_normal
    s = mx_kscale(K)[:, None]
    packed_xT = pack_weight(n((K, T)) * s)
    packed_w1 = pack_weight(n((K, H)) / np.sqrt(K) / s)
    perm = np.stack([np.random.permutation(S) for _ in range(8)])
    return {
        "x_words": packed_xT[0],
        "x_scales": packed_xT[1],
        "w1_words": packed_w1[0],
        "w1_scales": packed_w1[1],
        "gs": (np.random.uniform(0.5, 1.5, (K, 1)) / s).astype(np.float32),
        "tab": n((C, J)).astype(np.float32),
        "offs": striped8(np.random.randint(0, T, (8, S))),
        "n1": striped8(perm[:, :W]),
        "n2": striped8(perm[:, W:]),
        "cand": striped8(np.random.randint(0, T, (8, C))),
        "n3": striped8(np.random.randint(0, J, (8, S))),
        "n4": striped8(np.stack([np.random.permutation(S) for _ in range(8)])),
    }


def reference(x_words, x_scales, w1_words, w1_scales, gs, tab, offs, n1, n2, cand, n3, n4):
    x_cand = unpack_weight(x_words, x_scales)[np.arange(K)[:, None], runs(cand, K)]
    xq = unpack_weight(x_words, x_scales)[np.arange(K)[:, None], runs(offs, K)]
    y = unpack_weight(w1_words, w1_scales).T @ xq
    pa = y[np.arange(H)[:, None], runs(n1, H)]
    pb = y[np.arange(H)[:, None], runs(n2, H)]
    rb = np.minimum(pa, pb)
    ra = np.maximum(pa, pb)
    ds = np.zeros((H, S))
    ds[np.arange(H)[:, None], runs(n1, H)] = ra
    dt = ds.copy()
    dt[np.arange(H)[:, None], runs(n2, H)] = rb
    z = f64(gs) * dt
    s = 0.0625 * ((x_cand.T @ mxq(z, 0, "e4m3")))
    out_0 = np.maximum(s + f64(tab)[np.arange(C)[:, None], runs(n3, C)], s[np.arange(C)[:, None], runs(n4, C)])
    return (out_0,) + planes(out_0)

@@ -1,0 +1,193 @@
+from contextlib import ExitStack
+
+import concourse.mybir as mybir
+
+F32 = mybir.dt.float32
+BF16 = mybir.dt.bfloat16
+I32 = mybir.dt.int32
+U32 = mybir.dt.uint32
+U16 = mybir.dt.uint16
+U8 = mybir.dt.uint8
+FP8X4 = mybir.dt.float8_e4m3fn_x4
+ALU = mybir.AluOpType
+COPY = mybir.ActivationFunctionType.Copy
+
+P = 128
+PACK = 4
+T = 2048
+S = 512
+W = 256
+QUAD = 32
+FLOPS = 2 * 2 * 512 * 512 * 512
+HALVES = [(0, 256), (256, 512)]
+CHUNKS = [(0, 256), (256, 384), (384, 512)]
+
+
+def deal(nc, dst, src, run):
+    nc.vector.tensor_copy(
+        out=dst.rearrange("p (t b i) -> p b t i", t=PACK, i=run),
+        in_=src.rearrange("p (b i t) -> p b t i", t=PACK, i=run),
+    )
+
+
+def tile_picked_hcandorderkind_none_po_kernel(
+    tc, x_words, x_scales, w1_words, w1_scales, gs, tab, offs, n1, n2, cand, n3, n4, out_0, out_1, out_2
+):
+    nc = tc.nc
+    with ExitStack() as ctx:
+        lists = ctx.enter_context(tc.tile_pool(name="lists", bufs=1))
+        keep = ctx.enter_context(tc.tile_pool(name="keep", bufs=1))
+        psum = ctx.enter_context(tc.psum_pool(name="psum", bufs=1))
+
+        def sb(name, shape, dtype, tag=None):
+            return keep.tile(shape, dtype, name=name, tag=tag or name, align_bytes=64)
+
+        def load_list(name, src):
+            held = lists.tile(list(src.shape), U16, name=name)
+            nc.sync.dma_start(held[:], src)
+            return held
+
+        x_bytes = sb("x_bytes", [P, T], U8)
+        w_bytes = sb("w_bytes", [P, S], U8)
+        xq_scale = sb("xq_scale", [P, S], U8)
+        xc_scale = sb("xc_scale", [P, S], U8)
+        nc.vector.memset(x_bytes[:].bitcast(I32), 0)
+        for plane in (w_bytes, xq_scale, xc_scale):
+            nc.gpsimd.memset(plane[:].bitcast(I32), 0)
+
+        offs_sb = load_list("offs_sb", offs)
+        nc.sync.dma_start(x_bytes[0:P:8, :].bitcast(I32), x_scales[0].bitcast(I32))
+        w_raw = sb("w_raw", [P, S], I32)
+        nc.sync.dma_start(w_raw[:], w1_words[0].rearrange("p n t -> p (n t)").bitcast(I32))
+        x_table = sb("x_table", [P, T], I32)
+        nc.sync.dma_start(x_table[:], x_words[0].rearrange("p n t -> p (n t)").bitcast(I32))
+        for q in range(4):
+            nc.scalar.dma_start(
+                w_bytes[QUAD * q : QUAD * q + 4, :].bitcast(I32), w1_scales[0, 4 * q : 4 * q + 4, :].bitcast(I32)
+            )
+        cand_sb = load_list("cand_sb", cand)
+        n1_sb = load_list("n1_sb", n1)
+        n2_sb = load_list("n2_sb", n2)
+        gs_sb = sb("gs_sb", [P, PACK], F32)
+        nc.sync.dma_start(gs_sb[:], gs.rearrange("(p t) o -> p (t o)", t=PACK))
+        n3_sb = load_list("n3_sb", n3)
+        n4_sb = load_list("n4_sb", n4)
+
+        def place_scale_rows(engine, dst, src):
+            for r in range(4):
+                engine.dma_start(dst[r:P:QUAD, :].bitcast(I32), src[8 * r : P : QUAD, :].bitcast(I32))
+
+        xq_bytes = sb("xq_bytes", [P, S], U8)
+        nc.vector.tensor_copy(xq_bytes[:], x_bytes[:].indirect(offs_sb[:]))
+        place_scale_rows(nc.scalar, xq_scale, xq_bytes)
+        xc_bytes = sb("xc_bytes", [P, S], U8)
+        nc.vector.tensor_copy(xc_bytes[:], x_bytes[:].indirect(cand_sb[:]))
+        w_codes = sb("w_codes", [P, S], I32)
+        deal(nc, w_codes[:], w_raw[:], 4)
+        w_scale = sb("w_scale", [P, S], U8)
+        deal(nc, w_scale[:], w_bytes[:], 16)
+        xq_codes = sb("xq_codes", [P, S], U32)
+        nc.vector.tensor_copy(xq_codes[:], x_table[:].bitcast(U32).indirect(offs_sb[:]))
+
+        y = []
+        for t in range(PACK):
+            rows = slice(t * P, (t + 1) * P)
+            bank = psum.tile([P, S], F32, name=f"y_bank{t}")
+            nc.tensor.matmul_mx(
+                out=bank[:], lhsT=w_codes[:, rows].bitcast(FP8X4), lhsT_scale=w_scale[:, rows],
+                rhs=xq_codes[:].bitcast(FP8X4), rhs_scale=xq_scale[:], start=True, stop=True,
+            )
+            y_t = sb(f"y{t}", [P, S], F32)
+            nc.scalar.copy(y_t[:], bank[:])
+            y.append(y_t)
+
+        xc_words = sb("xc_words", [P, S], U32)
+        nc.vector.tensor_copy(xc_words[:], x_table[:].bitcast(U32).indirect(cand_sb[:]))
+        xc_dealt = sb("xc_dealt", [P, S], U8)
+        deal(nc, xc_dealt[:], xc_bytes[:], 16)
+        place_scale_rows(nc.sync, xc_scale, xc_dealt)
+        xc_codes = sb("xc_codes", [P, S], I32)
+        deal(nc, xc_codes[:], xc_words[:].bitcast(I32), 4)
+
+        tab_rows = tab.rearrange("(p t) j -> p t j", t=PACK)
+        tab_sb = []
+        for t in range(PACK):
+            tab_t = sb(f"tab{t}", [P, S], F32)
+            nc.sync.dma_start(tab_t[:], tab_rows[:, t, :])
+            tab_sb.append(tab_t)
+
+        z_bf = [sb(f"z_bf{h}", [P, hi - lo, PACK], BF16) for h, (lo, hi) in enumerate(HALVES)]
+        for pair in ((0, 1), (2, 3)):
+            picked = {t: sb(f"picked{t}", [P, 2, W], F32) for t in pair}
+            ordered = {t: sb(f"ordered{t}", [P, 2, W], F32, tag=f"slot{t}") for t in pair}
+            dt = {t: sb(f"dt{t}", [P, S], F32) for t in pair}
+            for t in pair:
+                nc.vector.tensor_copy(picked[t][:, 0, :], y[t][:].indirect(n1_sb[:]))
+                nc.vector.tensor_copy(picked[t][:, 1, :], y[t][:].indirect(n2_sb[:]))
+            for t in pair:
+                nc.vector.tensor_tensor(ordered[t][:, 0, :], picked[t][:, 0, :], picked[t][:, 1, :], ALU.max)
+                nc.vector.tensor_tensor(ordered[t][:, 1, :], picked[t][:, 0, :], picked[t][:, 1, :], ALU.min)
+            for side, places in enumerate((n1_sb, n2_sb)):
+                for t in pair:
+                    nc.vector.tensor_copy(dt[t][:].indirect(places[:]), ordered[t][:, side, :])
+            for t in pair:
+                for h, (lo, hi) in enumerate(HALVES):
+                    nc.scalar.activation(z_bf[h][:, :, t], dt[t][:, lo:hi], COPY, scale=gs_sb[:, t : t + 1])
+
+        z_codes = [sb(f"z_codes{h}", [P, hi - lo], U32) for h, (lo, hi) in enumerate(HALVES)]
+        z_scale = [sb(f"z_scale{h}", [P, hi - lo], U8) for h, (lo, hi) in enumerate(HALVES)]
+        s_banks = [psum.tile([P, S], F32, name=f"s_bank{t}") for t in range(PACK)]
+        for h, (lo, hi) in enumerate(HALVES):
+            nc.vector.quantize_mx(
+                out=z_codes[h][:].bitcast(FP8X4), scales=z_scale[h][:], in_=z_bf[h][:].rearrange("p n t -> p (n t)")
+            )
+            for t in range(PACK):
+                rows = slice(t * P, (t + 1) * P)
+                nc.tensor.matmul_mx(
+                    out=s_banks[t][:, lo:hi], lhsT=xc_codes[:, rows].bitcast(FP8X4), lhsT_scale=xc_scale[:, rows],
+                    rhs=z_codes[h][:].bitcast(FP8X4), rhs_scale=z_scale[h][:], start=True, stop=True,
+                )
+
+        kinds = [sb(f"kinds{i}", [P, 2, S], F32, tag=f"slot{2 + i}") for i in range(2)]
+        for t in range(PACK):
+            for lo, hi in HALVES:
+                nc.vector.tensor_copy(kinds[t // 2][:, t % 2, lo:hi], tab_sb[t][:].indirect(n3_sb[:, lo // 16 : hi // 16]))
+
+        s = []
+        for t in range(PACK):
+            s_t = sb(f"s{t}", [P, S], F32)
+            nc.scalar.activation(s_t[:], s_banks[t][:], COPY, scale=0.0625)
+            s.append(s_t)
+
+        first = sb("first", [P, PACK, S], F32)
+        out_rows = out_0.rearrange("(p t) j -> p t j", t=PACK)
+        out_words = out_1[0].rearrange("p n t -> p (n t)").bitcast(I32)
+        out_scale = sb("out_scale", [P, S], U8)
+        for c, (lo, hi) in enumerate(CHUNKS):
+            width = hi - lo
+            second = sb(f"second{c}", [P, PACK, width], F32)
+            for t in range(PACK):
+                nc.vector.tensor_copy(second[:, t, :], s[t][:].indirect(n4_sb[:, lo // 16 : hi // 16]))
+                if c == 0:
+                    nc.vector.tensor_tensor(first[:, t, :], s[t][:], kinds[t // 2][:, t % 2, :], ALU.add)
+            result = sb(f"result{c}", [P, PACK, width], F32)
+            nc.vector.tensor_tensor(result[:], first[:, :, lo:hi], second[:], ALU.max)
+            nc.sync.dma_start(out_rows[:, :, lo:hi], result[:])
+            result_bf = sb(f"result_bf{c}", [P, width, PACK], BF16)
+            dst = result_bf[:].rearrange("p (b i) t -> p b t i", i=4)
+            src = result[:].rearrange("p t (b i) -> p b t i", i=4)
+            if c == len(CHUNKS) - 1:
+                nc.vector.tensor_copy(dst, src)
+            else:
+                nc.scalar.copy(dst, src)
+            out_codes = sb(f"out_codes{c}", [P, width], I32)
+            nc.vector.quantize_mx(
+                out=out_codes[:].bitcast(FP8X4), scales=out_scale[:, lo:hi],
+                in_=result_bf[:].rearrange("p n t -> p (n t)"),
+            )
+            nc.scalar.dma_start(out_words[:, lo:hi], out_codes[:])
+        for q in range(4):
+            engine = nc.sync if q % 2 == 0 else nc.scalar
+            engine.dma_start(
+                out_2[0, 4 * q : 4 * q + 4, :].bitcast(I32), out_scale[QUAD * q : QUAD * q + 4, :].bitcast(I32)
+            )

@@ -1,6 +1,7 @@
 from contextlib import ExitStack
 
 import concourse.mybir as mybir
+from concourse.masks import make_identity
 
 F32 = mybir.dt.float32
 BF16 = mybir.dt.bfloat16
@@ -23,8 +24,8 @@ HALVES = [(0, 256), (256, 512)]
 CHUNKS = [(0, 256), (256, 384), (384, 512)]
 
 
-def deal(nc, dst, src, run):
-    nc.vector.tensor_copy(
+def deal(engine, dst, src, run):
+    engine.tensor_copy(
         out=dst.rearrange("p (t b i) -> p b t i", t=PACK, i=run),
         in_=src.rearrange("p (b i t) -> p b t i", t=PACK, i=run),
     )
@@ -47,68 +48,67 @@ def tile_picked_hcandorderkind_none_po_kernel(
             nc.sync.dma_start(held[:], src)
             return held
 
-        x_bytes = sb("x_bytes", [P, T], U8)
+        x_bytes = sb("x_bytes", [P, T], U8, tag="tab0")
         w_bytes = sb("w_bytes", [P, S], U8)
-        xq_scale = sb("xq_scale", [P, S], U8)
-        xc_scale = sb("xc_scale", [P, S], U8)
+        w_raw = sb("w_raw", [P, S], I32, tag="tab2")
+        x_table = sb("x_table", [P, T], I32, tag="tab3")
         nc.vector.memset(x_bytes[:].bitcast(I32), 0)
-        for plane in (w_bytes, xq_scale, xc_scale):
-            nc.gpsimd.memset(plane[:].bitcast(I32), 0)
+        nc.gpsimd.memset(w_bytes[:].bitcast(I32), 0)
+        ident = sb("ident", [P, P], F32)
+        make_identity(nc, ident[:])
 
         offs_sb = load_list("offs_sb", offs)
-        nc.sync.dma_start(x_bytes[0:P:8, :].bitcast(I32), x_scales[0].bitcast(I32))
-        w_raw = sb("w_raw", [P, S], I32)
         nc.sync.dma_start(w_raw[:], w1_words[0].rearrange("p n t -> p (n t)").bitcast(I32))
-        x_table = sb("x_table", [P, T], I32)
-        nc.sync.dma_start(x_table[:], x_words[0].rearrange("p n t -> p (n t)").bitcast(I32))
-        for q in range(4):
-            nc.scalar.dma_start(
-                w_bytes[QUAD * q : QUAD * q + 4, :].bitcast(I32), w1_scales[0, 4 * q : 4 * q + 4, :].bitcast(I32)
-            )
+        for e, engine in enumerate((nc.sync, nc.scalar)):
+            engine.dma_start(x_bytes[e:P:16, :].bitcast(I32), x_scales[0, e:16:2, :].bitcast(I32))
+        for e in range(2):
+            nc.scalar.dma_start(w_bytes[e:P:16, :].bitcast(I32), w1_scales[0, e:16:2, :].bitcast(I32))
         cand_sb = load_list("cand_sb", cand)
         n1_sb = load_list("n1_sb", n1)
+        nc.sync.dma_start(x_table[:], x_words[0].rearrange("p n t -> p (n t)").bitcast(I32))
         n2_sb = load_list("n2_sb", n2)
-        gs_sb = sb("gs_sb", [P, PACK], F32)
-        nc.sync.dma_start(gs_sb[:], gs.rearrange("(p t) o -> p (t o)", t=PACK))
         n3_sb = load_list("n3_sb", n3)
         n4_sb = load_list("n4_sb", n4)
 
-        def place_scale_rows(engine, dst, src):
-            for r in range(4):
-                engine.dma_start(dst[r:P:QUAD, :].bitcast(I32), src[8 * r : P : QUAD, :].bitcast(I32))
+        def place_odd_rows(plane, engines):
+            for e, engine in enumerate(engines):
+                engine.dma_start(plane[2 + e : P : QUAD].bitcast(I32), plane[16 + e : P : QUAD].bitcast(I32))
 
+        y_scales = sb("y_scales", [P, 2, S], U8)
+        deal(nc.vector, y_scales[:, 1, :], w_bytes[:], 16)
         xq_bytes = sb("xq_bytes", [P, S], U8)
         nc.vector.tensor_copy(xq_bytes[:], x_bytes[:].indirect(offs_sb[:]))
-        place_scale_rows(nc.scalar, xq_scale, xq_bytes)
-        xc_bytes = sb("xc_bytes", [P, S], U8)
-        nc.vector.tensor_copy(xc_bytes[:], x_bytes[:].indirect(cand_sb[:]))
+        nc.vector.tensor_copy(y_scales[:, 0, :].bitcast(I32), xq_bytes[:].bitcast(I32))
+        place_odd_rows(y_scales, (nc.sync, nc.scalar))
         w_codes = sb("w_codes", [P, S], I32)
-        deal(nc, w_codes[:], w_raw[:], 4)
-        w_scale = sb("w_scale", [P, S], U8)
-        deal(nc, w_scale[:], w_bytes[:], 16)
+        deal(nc.vector, w_codes[:], w_raw[:], 4)
         xq_codes = sb("xq_codes", [P, S], U32)
         nc.vector.tensor_copy(xq_codes[:], x_table[:].bitcast(U32).indirect(offs_sb[:]))
 
         y = []
         for t in range(PACK):
             rows = slice(t * P, (t + 1) * P)
-            bank = psum.tile([P, S], F32, name=f"y_bank{t}")
+            bank = psum.tile([P, S], F32, name=f"y_bank{t}", tag=f"y_bank{t}")
             nc.tensor.matmul_mx(
-                out=bank[:], lhsT=w_codes[:, rows].bitcast(FP8X4), lhsT_scale=w_scale[:, rows],
-                rhs=xq_codes[:].bitcast(FP8X4), rhs_scale=xq_scale[:], start=True, stop=True,
+                out=bank[:], lhsT=w_codes[:, rows].bitcast(FP8X4), lhsT_scale=y_scales[:, 1, rows],
+                rhs=xq_codes[:].bitcast(FP8X4), rhs_scale=y_scales[:, 0, :], start=True, stop=True,
             )
             y_t = sb(f"y{t}", [P, S], F32)
             nc.scalar.copy(y_t[:], bank[:])
             y.append(y_t)
 
-        xc_words = sb("xc_words", [P, S], U32)
+        xc_bytes = sb("xc_bytes", [P, S], U8, tag="tab1")
+        nc.vector.tensor_copy(xc_bytes[:], x_bytes[:].indirect(cand_sb[:]))
+        xc_words = sb("xc_words", [P, S], U32, tag="gs_sb")
         nc.vector.tensor_copy(xc_words[:], x_table[:].bitcast(U32).indirect(cand_sb[:]))
-        xc_dealt = sb("xc_dealt", [P, S], U8)
-        deal(nc, xc_dealt[:], xc_bytes[:], 16)
-        place_scale_rows(nc.sync, xc_scale, xc_dealt)
+        xc_scale = sb("xc_scale", [P, S], U8)
+        deal(nc.vector, xc_scale[:], xc_bytes[:], 16)
+        place_odd_rows(xc_scale, (nc.sync, nc.sync))
         xc_codes = sb("xc_codes", [P, S], I32)
-        deal(nc, xc_codes[:], xc_words[:].bitcast(I32), 4)
+        deal(nc.vector, xc_codes[:], xc_words[:].bitcast(I32), 4)
 
+        gs_sb = sb("gs_sb", [P, PACK], F32)
+        nc.sync.dma_start(gs_sb[:], gs.rearrange("(p t) o -> p (t o)", t=PACK))
         tab_rows = tab.rearrange("(p t) j -> p t j", t=PACK)
         tab_sb = []
         for t in range(PACK):
@@ -117,26 +117,29 @@ def tile_picked_hcandorderkind_none_po_kernel(
             tab_sb.append(tab_t)
 
         z_bf = [sb(f"z_bf{h}", [P, hi - lo, PACK], BF16) for h, (lo, hi) in enumerate(HALVES)]
-        for pair in ((0, 1), (2, 3)):
-            picked = {t: sb(f"picked{t}", [P, 2, W], F32) for t in pair}
-            ordered = {t: sb(f"ordered{t}", [P, 2, W], F32, tag=f"slot{t}") for t in pair}
+        picked = sb("picked", [P, PACK, 2, W], F32)
+        for t in range(PACK):
+            for side, places in enumerate((n1_sb, n2_sb)):
+                nc.vector.tensor_copy(picked[:, t, side, :], y[t][:].indirect(places[:]))
+        ordered = [sb(f"ordered{i}", [P, 2, 2, W], F32, tag=f"slot{i}") for i in range(2)]
+        for i in range(2):
+            for side, op in enumerate((ALU.max, ALU.min)):
+                nc.vector.tensor_tensor(
+                    ordered[i][:, :, side, :], picked[:, 2 * i : 2 * i + 2, 0, :], picked[:, 2 * i : 2 * i + 2, 1, :], op
+                )
+        for i in range(2):
+            pair = (2 * i, 2 * i + 1)
             dt = {t: sb(f"dt{t}", [P, S], F32) for t in pair}
-            for t in pair:
-                nc.vector.tensor_copy(picked[t][:, 0, :], y[t][:].indirect(n1_sb[:]))
-                nc.vector.tensor_copy(picked[t][:, 1, :], y[t][:].indirect(n2_sb[:]))
-            for t in pair:
-                nc.vector.tensor_tensor(ordered[t][:, 0, :], picked[t][:, 0, :], picked[t][:, 1, :], ALU.max)
-                nc.vector.tensor_tensor(ordered[t][:, 1, :], picked[t][:, 0, :], picked[t][:, 1, :], ALU.min)
             for side, places in enumerate((n1_sb, n2_sb)):
                 for t in pair:
-                    nc.vector.tensor_copy(dt[t][:].indirect(places[:]), ordered[t][:, side, :])
+                    nc.vector.tensor_copy(dt[t][:].indirect(places[:]), ordered[i][:, t % 2, side, :])
             for t in pair:
                 for h, (lo, hi) in enumerate(HALVES):
                     nc.scalar.activation(z_bf[h][:, :, t], dt[t][:, lo:hi], COPY, scale=gs_sb[:, t : t + 1])
 
         z_codes = [sb(f"z_codes{h}", [P, hi - lo], U32) for h, (lo, hi) in enumerate(HALVES)]
         z_scale = [sb(f"z_scale{h}", [P, hi - lo], U8) for h, (lo, hi) in enumerate(HALVES)]
-        s_banks = [psum.tile([P, S], F32, name=f"s_bank{t}") for t in range(PACK)]
+        s_banks = [psum.tile([P, S], F32, name=f"s_bank{t}", tag=f"s_bank{t}") for t in range(PACK)]
         for h, (lo, hi) in enumerate(HALVES):
             nc.vector.quantize_mx(
                 out=z_codes[h][:].bitcast(FP8X4), scales=z_scale[h][:], in_=z_bf[h][:].rearrange("p n t -> p (n t)")
@@ -148,10 +151,13 @@ def tile_picked_hcandorderkind_none_po_kernel(
                     rhs=z_codes[h][:].bitcast(FP8X4), rhs_scale=z_scale[h][:], start=True, stop=True,
                 )
 
-        kinds = [sb(f"kinds{i}", [P, 2, S], F32, tag=f"slot{2 + i}") for i in range(2)]
-        for t in range(PACK):
-            for lo, hi in HALVES:
-                nc.vector.tensor_copy(kinds[t // 2][:, t % 2, lo:hi], tab_sb[t][:].indirect(n3_sb[:, lo // 16 : hi // 16]))
+        kinds = {}
+        for name, h, tiles in (("slot1", 0, (0, 1)), ("z_bf0", 0, (2, 3)), ("z_bf1", 1, (0, 1, 2, 3))):
+            lo, hi = HALVES[h]
+            held = sb(f"kinds_{name}", [P, len(tiles), hi - lo], F32, tag=name)
+            for i, t in enumerate(tiles):
+                nc.vector.tensor_copy(held[:, i, :], tab_sb[t][:].indirect(n3_sb[:, lo // 16 : hi // 16]))
+                kinds[h, t] = held[:, i, :]
 
         s = []
         for t in range(PACK):
@@ -159,20 +165,41 @@ def tile_picked_hcandorderkind_none_po_kernel(
             nc.scalar.activation(s_t[:], s_banks[t][:], COPY, scale=0.0625)
             s.append(s_t)
 
-        first = sb("first", [P, PACK, S], F32)
+        turned = [psum.tile([P, PACK, P], F32, name=f"turned{b}", tag=f"y_bank{b}") for b in range(PACK)]
+        first = []
+        for h, (lo, hi) in enumerate(HALVES):
+            blocks = range(lo // P, hi // P)
+            terms = [[kinds[h, t] for t in range(PACK)], [s[t][:, lo:hi] for t in range(PACK)]]
+            if lo > 0:
+                terms.reverse()
+            for i, term in enumerate(terms):
+                for t in range(PACK):
+                    for b in blocks:
+                        nc.tensor.matmul(
+                            turned[b][:, t, :], term[t][:, b * P - lo : (b + 1) * P - lo], ident[:],
+                            start=(i == 0 and t == 0), stop=(i == 1 and t == PACK - 1), is_transpose=True,
+                        )
+            for b in blocks:
+                turned_sb = sb(f"turned_sb{b}", [P, PACK, P], F32)
+                nc.scalar.copy(turned_sb[:], turned[b][:])
+                bank = psum.tile([P, PACK, P], F32, name=f"first{b}", tag=f"s_bank{b}")
+                for t in range(PACK):
+                    nc.tensor.transpose(bank[:, t, :], turned_sb[:, t, :], ident[:])
+                first.append(bank)
+
         out_rows = out_0.rearrange("(p t) j -> p t j", t=PACK)
         out_words = out_1[0].rearrange("p n t -> p (n t)").bitcast(I32)
         out_scale = sb("out_scale", [P, S], U8)
         for c, (lo, hi) in enumerate(CHUNKS):
             width = hi - lo
-            second = sb(f"second{c}", [P, PACK, width], F32)
+            second = sb(f"second{c}", [P, PACK, width], F32, tag=f"second{c % 2}")
             for t in range(PACK):
                 nc.vector.tensor_copy(second[:, t, :], s[t][:].indirect(n4_sb[:, lo // 16 : hi // 16]))
-                if c == 0:
-                    nc.vector.tensor_tensor(first[:, t, :], s[t][:], kinds[t // 2][:, t % 2, :], ALU.add)
             result = sb(f"result{c}", [P, PACK, width], F32)
-            nc.vector.tensor_tensor(result[:], first[:, :, lo:hi], second[:], ALU.max)
-            nc.sync.dma_start(out_rows[:, :, lo:hi], result[:])
+            for b in range(lo // P, hi // P):
+                cols = slice(b * P - lo, (b + 1) * P - lo)
+                nc.vector.tensor_tensor(result[:, :, cols], first[b][:], second[:, :, cols], ALU.max)
+                nc.sync.dma_start(out_rows[:, :, b * P : (b + 1) * P], result[:, :, cols])
             result_bf = sb(f"result_bf{c}", [P, width, PACK], BF16)
             dst = result_bf[:].rearrange("p (b i) t -> p b t i", i=4)
             src = result[:].rearrange("p t (b i) -> p b t i", i=4)
@@ -185,7 +212,7 @@ def tile_picked_hcandorderkind_none_po_kernel(
                 out=out_codes[:].bitcast(FP8X4), scales=out_scale[:, lo:hi],
                 in_=result_bf[:].rearrange("p n t -> p (n t)"),
             )
-            nc.scalar.dma_start(out_words[:, lo:hi], out_codes[:])
+            (nc.scalar if c == len(CHUNKS) - 1 else nc.sync).dma_start(out_words[:, lo:hi], out_codes[:])
         for q in range(4):
             engine = nc.sync if q % 2 == 0 else nc.scalar
             engine.dma_start(

@@ -21,7 +21,6 @@ W = 256
 QUAD = 32
 FLOPS = 2 * 2 * 512 * 512 * 512
 HALVES = [(0, 256), (256, 512)]
-CHUNKS = [(0, 256), (256, 384), (384, 512)]
 
 
 def deal(engine, dst, src, run):
@@ -48,9 +47,9 @@ def tile_picked_hcandorderkind_none_po_kernel(
             nc.sync.dma_start(held[:], src)
             return held
 
-        x_bytes = sb("x_bytes", [P, T], U8, tag="tab0")
+        x_bytes = sb("x_bytes", [P, T], U8, tag="tab1")
         w_bytes = sb("w_bytes", [P, S], U8)
-        w_raw = sb("w_raw", [P, S], I32, tag="tab2")
+        w_raw = sb("w_raw", [P, S], I32)
         x_table = sb("x_table", [P, T], I32, tag="tab3")
         nc.vector.memset(x_bytes[:].bitcast(I32), 0)
         nc.gpsimd.memset(w_bytes[:].bitcast(I32), 0)
@@ -75,9 +74,9 @@ def tile_picked_hcandorderkind_none_po_kernel(
                 engine.dma_start(plane[2 + e : P : QUAD].bitcast(I32), plane[16 + e : P : QUAD].bitcast(I32))
 
         y_scales = sb("y_scales", [P, 2, S], U8)
-        deal(nc.vector, y_scales[:, 1, :], w_bytes[:], 16)
-        xq_bytes = sb("xq_bytes", [P, S], U8)
+        xq_bytes = sb("xq_bytes", [P, S], U8, tag="tab0")
         nc.vector.tensor_copy(xq_bytes[:], x_bytes[:].indirect(offs_sb[:]))
+        deal(nc.vector, y_scales[:, 1, :], w_bytes[:], 16)
         nc.vector.tensor_copy(y_scales[:, 0, :].bitcast(I32), xq_bytes[:].bitcast(I32))
         place_odd_rows(y_scales, (nc.sync, nc.scalar))
         w_codes = sb("w_codes", [P, S], I32)
@@ -97,7 +96,7 @@ def tile_picked_hcandorderkind_none_po_kernel(
             nc.scalar.copy(y_t[:], bank[:])
             y.append(y_t)
 
-        xc_bytes = sb("xc_bytes", [P, S], U8, tag="tab1")
+        xc_bytes = sb("xc_bytes", [P, S], U8, tag="tab2")
         nc.vector.tensor_copy(xc_bytes[:], x_bytes[:].indirect(cand_sb[:]))
         xc_words = sb("xc_words", [P, S], U32, tag="gs_sb")
         nc.vector.tensor_copy(xc_words[:], x_table[:].bitcast(U32).indirect(cand_sb[:]))
@@ -113,51 +112,58 @@ def tile_picked_hcandorderkind_none_po_kernel(
         tab_sb = []
         for t in range(PACK):
             tab_t = sb(f"tab{t}", [P, S], F32)
-            nc.sync.dma_start(tab_t[:], tab_rows[:, t, :])
+            (nc.scalar if t == 0 else nc.sync).dma_start(tab_t[:], tab_rows[:, t, :])
             tab_sb.append(tab_t)
 
-        z_bf = [sb(f"z_bf{h}", [P, hi - lo, PACK], BF16) for h, (lo, hi) in enumerate(HALVES)]
+        kinds = {}
+
+        def gather_kinds(name, tag, pieces):
+            held = sb(name, [P, len(pieces), W], F32, tag=tag)
+            for i, (h, t) in enumerate(pieces):
+                lo, hi = HALVES[h]
+                nc.vector.tensor_copy(held[:, i, :], tab_sb[t][:].indirect(n3_sb[:, lo // 16 : hi // 16]))
+                kinds[h, t] = held[:, i, :]
+
+        gather_kinds("kinds_early", None, [(0, 0), (1, 0)])
+
         picked = sb("picked", [P, PACK, 2, W], F32)
         for t in range(PACK):
             for side, places in enumerate((n1_sb, n2_sb)):
                 nc.vector.tensor_copy(picked[:, t, side, :], y[t][:].indirect(places[:]))
-        ordered = [sb(f"ordered{i}", [P, 2, 2, W], F32, tag=f"slot{i}") for i in range(2)]
+        ordered = {}
         for i in range(2):
             for side, op in enumerate((ALU.max, ALU.min)):
+                ordered[i, side] = sb(f"ordered{i}{side}", [P, 2, W], F32)
                 nc.vector.tensor_tensor(
-                    ordered[i][:, :, side, :], picked[:, 2 * i : 2 * i + 2, 0, :], picked[:, 2 * i : 2 * i + 2, 1, :], op
+                    ordered[i, side][:], picked[:, 2 * i : 2 * i + 2, 0, :], picked[:, 2 * i : 2 * i + 2, 1, :], op
                 )
+        z_bf = [sb(f"z_bf{h}", [P, W, PACK], BF16) for h in range(2)]
         for i in range(2):
             pair = (2 * i, 2 * i + 1)
             dt = {t: sb(f"dt{t}", [P, S], F32) for t in pair}
             for side, places in enumerate((n1_sb, n2_sb)):
                 for t in pair:
-                    nc.vector.tensor_copy(dt[t][:].indirect(places[:]), ordered[i][:, t % 2, side, :])
+                    nc.vector.tensor_copy(dt[t][:].indirect(places[:]), ordered[i, side][:, t % 2, :])
             for t in pair:
                 for h, (lo, hi) in enumerate(HALVES):
                     nc.scalar.activation(z_bf[h][:, :, t], dt[t][:, lo:hi], COPY, scale=gs_sb[:, t : t + 1])
 
-        z_codes = [sb(f"z_codes{h}", [P, hi - lo], U32) for h, (lo, hi) in enumerate(HALVES)]
-        z_scale = [sb(f"z_scale{h}", [P, hi - lo], U8) for h, (lo, hi) in enumerate(HALVES)]
+        gather_kinds("kinds_a", "dt1", [(0, 1), (0, 2)])
         s_banks = [psum.tile([P, S], F32, name=f"s_bank{t}", tag=f"s_bank{t}") for t in range(PACK)]
         for h, (lo, hi) in enumerate(HALVES):
+            z_codes = sb(f"z_codes{h}", [P, W], U32)
+            z_scale = sb(f"z_scale{h}", [P, W], U8)
             nc.vector.quantize_mx(
-                out=z_codes[h][:].bitcast(FP8X4), scales=z_scale[h][:], in_=z_bf[h][:].rearrange("p n t -> p (n t)")
+                out=z_codes[:].bitcast(FP8X4), scales=z_scale[:], in_=z_bf[h][:].rearrange("p n t -> p (n t)")
             )
             for t in range(PACK):
                 rows = slice(t * P, (t + 1) * P)
                 nc.tensor.matmul_mx(
                     out=s_banks[t][:, lo:hi], lhsT=xc_codes[:, rows].bitcast(FP8X4), lhsT_scale=xc_scale[:, rows],
-                    rhs=z_codes[h][:].bitcast(FP8X4), rhs_scale=z_scale[h][:], start=True, stop=True,
+                    rhs=z_codes[:].bitcast(FP8X4), rhs_scale=z_scale[:], start=True, stop=True,
                 )
-
-        kinds = {}
-        for name, h, tiles in (("slot1", 0, (0, 1)), ("z_bf0", 0, (2, 3)), ("z_bf1", 1, (0, 1, 2, 3))):
-            lo, hi = HALVES[h]
-            held = sb(f"kinds_{name}", [P, len(tiles), hi - lo], F32, tag=name)
-            for i, t in enumerate(tiles):
-                nc.vector.tensor_copy(held[:, i, :], tab_sb[t][:].indirect(n3_sb[:, lo // 16 : hi // 16]))
-                kinds[h, t] = held[:, i, :]
+        gather_kinds("kinds_b", "z_bf0", [(0, 3), (1, 1)])
+        gather_kinds("kinds_c", "dt3", [(1, 2), (1, 3)])
 
         s = []
         for t in range(PACK):
@@ -166,55 +172,60 @@ def tile_picked_hcandorderkind_none_po_kernel(
             s.append(s_t)
 
         turned = [psum.tile([P, PACK, P], F32, name=f"turned{b}", tag=f"y_bank{b}") for b in range(PACK)]
+        for b in range(PACK):
+            for t in range(PACK):
+                nc.tensor.matmul(
+                    turned[b][:, t, :], kinds[b // 2, t][:, b % 2 * P : (b % 2 + 1) * P], ident[:],
+                    start=(t == 0), stop=False, is_transpose=True,
+                )
+        for t in range(PACK):
+            for b in range(PACK):
+                nc.tensor.matmul(
+                    turned[b][:, t, :], s[t][:, b * P : (b + 1) * P], ident[:],
+                    start=False, stop=(t == PACK - 1), is_transpose=True,
+                )
         first = []
+        for b in range(PACK):
+            turned_sb = sb(f"turned_sb{b}", [P, PACK, P], F32)
+            nc.scalar.copy(turned_sb[:], turned[b][:])
+            bank = psum.tile([P, PACK, P], F32, name=f"first{b}", tag=f"s_bank{b}")
+            for t in range(PACK):
+                nc.tensor.transpose(bank[:, t, :], turned_sb[:, t, :], ident[:])
+            first.append(bank)
+
+        second = []
         for h, (lo, hi) in enumerate(HALVES):
-            blocks = range(lo // P, hi // P)
-            terms = [[kinds[h, t] for t in range(PACK)], [s[t][:, lo:hi] for t in range(PACK)]]
-            if lo > 0:
-                terms.reverse()
-            for i, term in enumerate(terms):
-                for t in range(PACK):
-                    for b in blocks:
-                        nc.tensor.matmul(
-                            turned[b][:, t, :], term[t][:, b * P - lo : (b + 1) * P - lo], ident[:],
-                            start=(i == 0 and t == 0), stop=(i == 1 and t == PACK - 1), is_transpose=True,
-                        )
-            for b in blocks:
-                turned_sb = sb(f"turned_sb{b}", [P, PACK, P], F32)
-                nc.scalar.copy(turned_sb[:], turned[b][:])
-                bank = psum.tile([P, PACK, P], F32, name=f"first{b}", tag=f"s_bank{b}")
-                for t in range(PACK):
-                    nc.tensor.transpose(bank[:, t, :], turned_sb[:, t, :], ident[:])
-                first.append(bank)
+            fetched = sb(f"second{h}", [P, PACK, W], F32)
+            for t in range(PACK):
+                nc.vector.tensor_copy(fetched[:, t, :], s[t][:].indirect(n4_sb[:, lo // 16 : hi // 16]))
+            second.append(fetched)
 
         out_rows = out_0.rearrange("(p t) j -> p t j", t=PACK)
         out_words = out_1[0].rearrange("p n t -> p (n t)").bitcast(I32)
         out_scale = sb("out_scale", [P, S], U8)
-        for c, (lo, hi) in enumerate(CHUNKS):
-            width = hi - lo
-            second = sb(f"second{c}", [P, PACK, width], F32, tag=f"second{c % 2}")
-            for t in range(PACK):
-                nc.vector.tensor_copy(second[:, t, :], s[t][:].indirect(n4_sb[:, lo // 16 : hi // 16]))
-            result = sb(f"result{c}", [P, PACK, width], F32)
-            for b in range(lo // P, hi // P):
-                cols = slice(b * P - lo, (b + 1) * P - lo)
-                nc.vector.tensor_tensor(result[:, :, cols], first[b][:], second[:, :, cols], ALU.max)
-                nc.sync.dma_start(out_rows[:, :, b * P : (b + 1) * P], result[:, :, cols])
-            result_bf = sb(f"result_bf{c}", [P, width, PACK], BF16)
-            dst = result_bf[:].rearrange("p (b i) t -> p b t i", i=4)
-            src = result[:].rearrange("p t (b i) -> p b t i", i=4)
-            if c == len(CHUNKS) - 1:
-                nc.vector.tensor_copy(dst, src)
-            else:
-                nc.scalar.copy(dst, src)
-            out_codes = sb(f"out_codes{c}", [P, width], I32)
+        for h, (lo, hi) in enumerate(HALVES):
+            result_bf = sb(f"result_bf{h}", [P, W, PACK], BF16)
+            for b in (2 * h, 2 * h + 1):
+                cols = slice(b % 2 * P, (b % 2 + 1) * P)
+                woven = result_bf[:, cols, :].rearrange("p (g i) t -> p g t i", i=4)
+                if b == PACK - 1:
+                    nc.vector.tensor_tensor(
+                        woven, first[b][:].rearrange("p t (g i) -> p g t i", i=4),
+                        second[h][:, :, cols].rearrange("p t (g i) -> p g t i", i=4), ALU.max,
+                    )
+                result = sb(f"result{b}", [P, PACK, P], F32)
+                nc.vector.tensor_tensor(result[:], first[b][:], second[h][:, :, cols], ALU.max)
+                nc.sync.dma_start(out_rows[:, :, b * P : (b + 1) * P], result[:])
+                if b < PACK - 1:
+                    nc.scalar.copy(woven, result[:].rearrange("p t (g i) -> p g t i", i=4))
+            out_codes = sb(f"out_codes{h}", [P, W], I32)
             nc.vector.quantize_mx(
                 out=out_codes[:].bitcast(FP8X4), scales=out_scale[:, lo:hi],
                 in_=result_bf[:].rearrange("p n t -> p (n t)"),
             )
-            (nc.scalar if c == len(CHUNKS) - 1 else nc.sync).dma_start(out_words[:, lo:hi], out_codes[:])
+            nc.sync.dma_start(out_words[:, lo:hi], out_codes[:])
         for q in range(4):
-            engine = nc.sync if q % 2 == 0 else nc.scalar
+            engine = nc.sync if q == 0 else nc.scalar
             engine.dma_start(
                 out_2[0, 4 * q : 4 * q + 4, :].bitcast(I32), out_scale[QUAD * q : QUAD * q + 4, :].bitcast(I32)
             )

from contextlib import ExitStack

import concourse.mybir as mybir
from concourse.masks import make_identity

F32 = mybir.dt.float32
BF16 = mybir.dt.bfloat16
I32 = mybir.dt.int32
U32 = mybir.dt.uint32
U16 = mybir.dt.uint16
U8 = mybir.dt.uint8
FP8X4 = mybir.dt.float8_e4m3fn_x4
ALU = mybir.AluOpType
COPY = mybir.ActivationFunctionType.Copy

P = 128
PACK = 4
T = 2048
S = 512
W = 256
QUAD = 32
FLOPS = 2 * 2 * 512 * 512 * 512
HALVES = [(0, 256), (256, 512)]


def deal(engine, dst, src, run):
    engine.tensor_copy(
        out=dst.rearrange("p (t b i) -> p b t i", t=PACK, i=run),
        in_=src.rearrange("p (b i t) -> p b t i", t=PACK, i=run),
    )


def tile_picked_hcandorderkind_none_po_kernel(
    tc, x_words, x_scales, w1_words, w1_scales, gs, tab, offs, n1, n2, cand, n3, n4, out_0, out_1, out_2
):
    nc = tc.nc
    with ExitStack() as ctx:
        lists = ctx.enter_context(tc.tile_pool(name="lists", bufs=1))
        keep = ctx.enter_context(tc.tile_pool(name="keep", bufs=1))
        psum = ctx.enter_context(tc.psum_pool(name="psum", bufs=1))

        def sb(name, shape, dtype, tag=None):
            return keep.tile(shape, dtype, name=name, tag=tag or name, align_bytes=64)

        def load_list(name, src):
            held = lists.tile(list(src.shape), U16, name=name)
            nc.sync.dma_start(held[:], src)
            return held

        x_bytes = sb("x_bytes", [P, T], U8, tag="tab1")
        w_bytes = sb("w_bytes", [P, S], U8)
        w_raw = sb("w_raw", [P, S], I32)
        x_table = sb("x_table", [P, T], I32, tag="tab3")
        nc.vector.memset(x_bytes[:].bitcast(I32), 0)
        nc.gpsimd.memset(w_bytes[:].bitcast(I32), 0)
        ident = sb("ident", [P, P], F32)
        make_identity(nc, ident[:])

        offs_sb = load_list("offs_sb", offs)
        nc.sync.dma_start(w_raw[:], w1_words[0].rearrange("p n t -> p (n t)").bitcast(I32))
        for e, engine in enumerate((nc.sync, nc.scalar)):
            engine.dma_start(x_bytes[e:P:16, :].bitcast(I32), x_scales[0, e:16:2, :].bitcast(I32))
        for e in range(2):
            nc.scalar.dma_start(w_bytes[e:P:16, :].bitcast(I32), w1_scales[0, e:16:2, :].bitcast(I32))
        cand_sb = load_list("cand_sb", cand)
        n1_sb = load_list("n1_sb", n1)
        nc.sync.dma_start(x_table[:], x_words[0].rearrange("p n t -> p (n t)").bitcast(I32))
        n2_sb = load_list("n2_sb", n2)
        n3_sb = load_list("n3_sb", n3)
        n4_sb = load_list("n4_sb", n4)

        def place_odd_rows(plane, engines):
            for e, engine in enumerate(engines):
                engine.dma_start(plane[2 + e : P : QUAD].bitcast(I32), plane[16 + e : P : QUAD].bitcast(I32))

        y_scales = sb("y_scales", [P, 2, S], U8)
        xq_bytes = sb("xq_bytes", [P, S], U8, tag="tab0")
        nc.vector.tensor_copy(xq_bytes[:], x_bytes[:].indirect(offs_sb[:]))
        deal(nc.vector, y_scales[:, 1, :], w_bytes[:], 16)
        nc.vector.tensor_copy(y_scales[:, 0, :].bitcast(I32), xq_bytes[:].bitcast(I32))
        place_odd_rows(y_scales, (nc.sync, nc.scalar))
        w_codes = sb("w_codes", [P, S], I32)
        deal(nc.vector, w_codes[:], w_raw[:], 4)
        xq_codes = sb("xq_codes", [P, S], U32)
        nc.vector.tensor_copy(xq_codes[:], x_table[:].bitcast(U32).indirect(offs_sb[:]))

        y = []
        for t in range(PACK):
            rows = slice(t * P, (t + 1) * P)
            bank = psum.tile([P, S], F32, name=f"y_bank{t}", tag=f"y_bank{t}")
            nc.tensor.matmul_mx(
                out=bank[:], lhsT=w_codes[:, rows].bitcast(FP8X4), lhsT_scale=y_scales[:, 1, rows],
                rhs=xq_codes[:].bitcast(FP8X4), rhs_scale=y_scales[:, 0, :], start=True, stop=True,
            )
            y_t = sb(f"y{t}", [P, S], F32)
            nc.scalar.copy(y_t[:], bank[:])
            y.append(y_t)

        xc_bytes = sb("xc_bytes", [P, S], U8, tag="tab2")
        nc.vector.tensor_copy(xc_bytes[:], x_bytes[:].indirect(cand_sb[:]))
        xc_words = sb("xc_words", [P, S], U32, tag="gs_sb")
        nc.vector.tensor_copy(xc_words[:], x_table[:].bitcast(U32).indirect(cand_sb[:]))
        xc_scale = sb("xc_scale", [P, S], U8)
        deal(nc.vector, xc_scale[:], xc_bytes[:], 16)
        place_odd_rows(xc_scale, (nc.sync, nc.sync))
        xc_codes = sb("xc_codes", [P, S], I32)
        deal(nc.vector, xc_codes[:], xc_words[:].bitcast(I32), 4)

        gs_sb = sb("gs_sb", [P, PACK], F32)
        nc.sync.dma_start(gs_sb[:], gs.rearrange("(p t) o -> p (t o)", t=PACK))
        tab_rows = tab.rearrange("(p t) j -> p t j", t=PACK)
        tab_sb = []
        for t in range(PACK):
            tab_t = sb(f"tab{t}", [P, S], F32)
            (nc.scalar if t == 0 else nc.sync).dma_start(tab_t[:], tab_rows[:, t, :])
            tab_sb.append(tab_t)

        kinds = {}

        def gather_kinds(name, tag, pieces):
            held = sb(name, [P, len(pieces), W], F32, tag=tag)
            for i, (h, t) in enumerate(pieces):
                lo, hi = HALVES[h]
                nc.vector.tensor_copy(held[:, i, :], tab_sb[t][:].indirect(n3_sb[:, lo // 16 : hi // 16]))
                kinds[h, t] = held[:, i, :]

        gather_kinds("kinds_early", None, [(0, 0), (1, 0)])

        picked = sb("picked", [P, PACK, 2, W], F32)
        for t in range(PACK):
            for side, places in enumerate((n1_sb, n2_sb)):
                nc.vector.tensor_copy(picked[:, t, side, :], y[t][:].indirect(places[:]))
        ordered = {}
        for i in range(2):
            for side, op in enumerate((ALU.max, ALU.min)):
                ordered[i, side] = sb(f"ordered{i}{side}", [P, 2, W], F32)
                nc.vector.tensor_tensor(
                    ordered[i, side][:], picked[:, 2 * i : 2 * i + 2, 0, :], picked[:, 2 * i : 2 * i + 2, 1, :], op
                )
        z_bf = [sb(f"z_bf{h}", [P, W, PACK], BF16) for h in range(2)]
        for i in range(2):
            pair = (2 * i, 2 * i + 1)
            dt = {t: sb(f"dt{t}", [P, S], F32) for t in pair}
            for side, places in enumerate((n1_sb, n2_sb)):
                for t in pair:
                    nc.vector.tensor_copy(dt[t][:].indirect(places[:]), ordered[i, side][:, t % 2, :])
            for t in pair:
                for h, (lo, hi) in enumerate(HALVES):
                    nc.scalar.activation(z_bf[h][:, :, t], dt[t][:, lo:hi], COPY, scale=gs_sb[:, t : t + 1])

        gather_kinds("kinds_a", "dt1", [(0, 1), (0, 2)])
        s_banks = [psum.tile([P, S], F32, name=f"s_bank{t}", tag=f"s_bank{t}") for t in range(PACK)]
        for h, (lo, hi) in enumerate(HALVES):
            z_codes = sb(f"z_codes{h}", [P, W], U32)
            z_scale = sb(f"z_scale{h}", [P, W], U8)
            nc.vector.quantize_mx(
                out=z_codes[:].bitcast(FP8X4), scales=z_scale[:], in_=z_bf[h][:].rearrange("p n t -> p (n t)")
            )
            for t in range(PACK):
                rows = slice(t * P, (t + 1) * P)
                nc.tensor.matmul_mx(
                    out=s_banks[t][:, lo:hi], lhsT=xc_codes[:, rows].bitcast(FP8X4), lhsT_scale=xc_scale[:, rows],
                    rhs=z_codes[:].bitcast(FP8X4), rhs_scale=z_scale[:], start=True, stop=True,
                )
        gather_kinds("kinds_b", "z_bf0", [(0, 3), (1, 1)])
        gather_kinds("kinds_c", "dt3", [(1, 2), (1, 3)])

        s = []
        for t in range(PACK):
            s_t = sb(f"s{t}", [P, S], F32)
            nc.scalar.activation(s_t[:], s_banks[t][:], COPY, scale=0.0625)
            s.append(s_t)

        turned = [psum.tile([P, PACK, P], F32, name=f"turned{b}", tag=f"y_bank{b}") for b in range(PACK)]
        for b in range(PACK):
            for t in range(PACK):
                nc.tensor.matmul(
                    turned[b][:, t, :], kinds[b // 2, t][:, b % 2 * P : (b % 2 + 1) * P], ident[:],
                    start=(t == 0), stop=False, is_transpose=True,
                )
        for t in range(PACK):
            for b in range(PACK):
                nc.tensor.matmul(
                    turned[b][:, t, :], s[t][:, b * P : (b + 1) * P], ident[:],
                    start=False, stop=(t == PACK - 1), is_transpose=True,
                )
        first = []
        for b in range(PACK):
            turned_sb = sb(f"turned_sb{b}", [P, PACK, P], F32)
            nc.scalar.copy(turned_sb[:], turned[b][:])
            bank = psum.tile([P, PACK, P], F32, name=f"first{b}", tag=f"s_bank{b}")
            for t in range(PACK):
                nc.tensor.transpose(bank[:, t, :], turned_sb[:, t, :], ident[:])
            first.append(bank)

        second = []
        for h, (lo, hi) in enumerate(HALVES):
            fetched = sb(f"second{h}", [P, PACK, W], F32)
            for t in range(PACK):
                nc.vector.tensor_copy(fetched[:, t, :], s[t][:].indirect(n4_sb[:, lo // 16 : hi // 16]))
            second.append(fetched)

        out_rows = out_0.rearrange("(p t) j -> p t j", t=PACK)
        out_words = out_1[0].rearrange("p n t -> p (n t)").bitcast(I32)
        out_scale = sb("out_scale", [P, S], U8)
        for h, (lo, hi) in enumerate(HALVES):
            result_bf = sb(f"result_bf{h}", [P, W, PACK], BF16)
            for b in (2 * h, 2 * h + 1):
                cols = slice(b % 2 * P, (b % 2 + 1) * P)
                woven = result_bf[:, cols, :].rearrange("p (g i) t -> p g t i", i=4)
                if b == PACK - 1:
                    nc.vector.tensor_tensor(
                        woven, first[b][:].rearrange("p t (g i) -> p g t i", i=4),
                        second[h][:, :, cols].rearrange("p t (g i) -> p g t i", i=4), ALU.max,
                    )
                result = sb(f"result{b}", [P, PACK, P], F32)
                nc.vector.tensor_tensor(result[:], first[b][:], second[h][:, :, cols], ALU.max)
                nc.sync.dma_start(out_rows[:, :, b * P : (b + 1) * P], result[:])
                if b < PACK - 1:
                    nc.scalar.copy(woven, result[:].rearrange("p t (g i) -> p g t i", i=4))
            out_codes = sb(f"out_codes{h}", [P, W], I32)
            nc.vector.quantize_mx(
                out=out_codes[:].bitcast(FP8X4), scales=out_scale[:, lo:hi],
                in_=result_bf[:].rearrange("p n t -> p (n t)"),
            )
            nc.sync.dma_start(out_words[:, lo:hi], out_codes[:])
        for q in range(4):
            engine = nc.sync if q == 0 else nc.scalar
            engine.dma_start(
                out_2[0, 4 * q : 4 * q + 4, :].bitcast(I32), out_scale[QUAD * q : QUAD * q + 4, :].bitcast(I32)
            )
